import numpy as np
import ml_dtypes


def mxq(x, axis, fmt="e4m3"):
    dtype, down = {"e4m3": (ml_dtypes.float8_e4m3fn, 7), "e5m2": (ml_dtypes.float8_e5m2, 14)}[fmt]
    v = np.moveaxis(np.asarray(x, np.float32).astype(ml_dtypes.bfloat16).astype(np.float64), axis, -1)
    blocks = v.reshape(v.shape[:-1] + (-1, 32))
    amax = np.abs(blocks).max(-1, keepdims=True)
    byte = np.maximum(np.where(amax > 0, np.frexp(amax)[1] - 1 + 127, 0) - down, 1)
    scale = np.exp2(byte - 127.0)
    codes = (blocks / scale).astype(np.float32).astype(dtype).astype(np.float64)
    return np.moveaxis((codes * scale).reshape(v.shape), -1, axis)


WIDE = False


def mx_kscale(k):
    if not WIDE:
        return np.ones(k)
    levels = np.array([10, -10, 5, -5, 0])
    if k % 512:
        return np.exp2(np.random.permutation(np.resize(levels, k // 32))).repeat(32)
    a = np.empty((k // 512, 16))
    for p in range(k // 512):
        a[p, :8] = np.random.permutation(np.resize(levels, 8))
        for g in range(8):
            far = levels[np.abs(levels - a[p, g]) >= 10]
            a[p, g + 8] = far[np.random.randint(len(far))]
    return np.exp2(a.ravel()).repeat(32)


def f64(x):
    return np.asarray(x).astype(np.float64)


def striped(idx):
    return np.tile(idx.reshape(-1, 16).T, (8, 1)).astype(np.uint16)


def unstriped(offs):
    return offs[:16].T.reshape(-1).astype(np.int64)


E2M1 = np.array([0.0, 0.5, 1.0, 1.5, 2.0, 3.0, 4.0, 6.0, -0.0, -0.5, -1.0, -1.5, -2.0, -3.0, -4.0, -6.0])


def pack_weight(w, fmt):
    k, n = w.shape
    w = f64(np.asarray(w, np.float32).astype(ml_dtypes.bfloat16)).reshape(k // 32, 32, n)
    amax = np.abs(w).max(1)
    if fmt == "e4m3":
        byte = np.frexp(amax)[1] - 1 + 127 - 7
    else:
        mant, ex = np.frexp(amax / 6.0)
        byte = np.where(mant > 0.5, ex, ex - 1) + 127
    byte = np.clip(np.where(amax > 0, byte, 1), 1, 254)
    scaled = (w * np.exp2(127.0 - byte)[:, None, :]).reshape(k, n).astype(np.float32)
    by_word = np.ascontiguousarray(scaled.reshape(k // 512, 128, 4, n).transpose(0, 1, 3, 2))
    if fmt == "e4m3":
        words = by_word.astype(ml_dtypes.float8_e4m3fn).view(np.uint8)
    else:
        c = by_word.astype(ml_dtypes.float4_e2m1fn).view(np.uint8) & 0xF
        words = (c[..., 0::2] | (c[..., 1::2] << 4)).reshape(k // 512, 128, 2 * n)
    return np.ascontiguousarray(words), np.ascontiguousarray(byte.astype(np.uint8).reshape(k // 512, 16, n))


def unpack_weight(words, scales, fmt):
    g, _, n = scales.shape
    words = np.ascontiguousarray(words).reshape(g, 128, n, -1)
    if fmt == "e4m3":
        vals = words.view(ml_dtypes.float8_e4m3fn).astype(np.float64)
    else:
        nib = np.empty((g, 128, n, 4), np.uint8)
        nib[..., 0::2] = words & 0xF
        nib[..., 1::2] = words >> 4
        vals = E2M1[nib]
    vals = vals * np.repeat(np.exp2(scales.astype(np.float64) - 127.0), 8, axis=1)[..., None]
    return vals.transpose(0, 1, 3, 2).reshape(g * 512, n)


def gelu(v):
    return 0.5 * v * (1.0 + np.tanh(np.sqrt(2.0 / np.pi) * (v + 0.044715 * v**3)))


K, H, T, S, T2, S2 = 512, 1024, 2048, 1024, 4096, 1024

def setup_inputs():
    n = np.random.standard_normal
    s = mx_kscale(K)[:, None]
    u = mx_kscale(H)[:, None]
    tab_words, tab_scales = pack_weight(n((K, T)) * s, "e4m3")
    tab2_words, tab2_scales = pack_weight(0.7 * n((H, T2)) / np.sqrt(H) / u, "e4m3")
    w4_words, w4_scales = pack_weight(n((K, H)) / np.sqrt(K) / s * u.T, "e2m1")
    w1 = (n((K, H)) / np.sqrt(K) / s).astype(np.float32)
    mean = (0.5 * n(S2)).astype(np.float32)
    offs = striped(np.random.permutation(T)[:S])
    offs2 = striped(np.random.permutation(T2)[:S2])
    return {"tab_words": tab_words, "tab_scales": tab_scales, "tab2_words": tab2_words, "tab2_scales": tab2_scales,
            "w4_words": w4_words, "w4_scales": w4_scales, "w1": w1, "mean": mean, "offs": offs, "offs2": offs2}

def reference(tab_words, tab_scales, tab2_words, tab2_scales, w4_words, w4_scales, w1, mean, offs, offs2):
    v = unpack_weight(tab_words, tab_scales, "e4m3")[:, unstriped(offs)]
    v2 = unpack_weight(tab2_words, tab2_scales, "e4m3")[:, unstriped(offs2)]
    w4 = unpack_weight(w4_words, w4_scales, "e2m1")
    x = mxq(f64(w1), 0, "e4m3").T @ v
    a = w4.T @ v
    h = a / (1.0 + x * x)
    y = v2.T @ mxq(h, 0, "e4m3")
    return np.exp(y + f64(mean)[:, None])

@@ -1,0 +1,258 @@
+from contextlib import ExitStack
+
+import concourse.mybir as mybir
+
+K, H, T, S, T2, S2 = 512, 1024, 2048, 1024, 4096, 1024
+FLOPS = 2 * K * H * S * 2 + 2 * H * S2 * S
+
+F32 = mybir.dt.float32
+BF16 = mybir.dt.bfloat16
+I32 = mybir.dt.int32
+U32 = mybir.dt.uint32
+U16 = mybir.dt.uint16
+U8 = mybir.dt.uint8
+FP8X4 = mybir.dt.float8_e4m3fn_x4
+FP4X4 = mybir.dt.float4_e2m1fn_x4
+ACT = mybir.ActivationFunctionType
+ALU = mybir.AluOpType
+
+P = 128
+PACK = 4
+PASS = P * PACK
+BLOCKS = H // PASS
+JC = 128
+CHUNKS = S // JC
+BANK = 512
+SLICE = 512
+FIRST = 256
+SHARE = 24
+SCALAR_STEPS = (7, 14)
+
+
+def tile_list_power_spectrum_emulator_kernel(
+    tc, tab_words, tab_scales, tab2_words, tab2_scales, w4_words, w4_scales, w1, mean, offs, offs2, out
+):
+    nc = tc.nc
+    with ExitStack() as ctx:
+        keep = ctx.enter_context(tc.tile_pool(name="keep", bufs=1))
+        ring = ctx.enter_context(tc.tile_pool(name="ring", bufs=4))
+        psum = ctx.enter_context(tc.psum_pool(name="psum", bufs=4))
+
+        def held(name, shape, dtype, tag=""):
+            return keep.tile(shape, dtype, name=name, tag=tag, align_bytes=64)
+
+        idx = keep.tile([P, S // 16], U16, name="idx")
+        idx2 = keep.tile([P, S2 // 16], U16, name="idx2")
+        tab_w = held("tab_w", [P, T], I32)
+        tab_s = held("tab_s", [P, T], U8)
+        w4_raw = held("w4_raw", [P, 2 * H], U8)
+        w4_raw_s = held("w4_raw_s", [P, H], U8)
+        w4_w = held("w4_w", [P, 2 * H], U8)
+        w4_s = held("w4_s", [P, H], U8)
+        v_w = held("v_w", [P, S], U32)
+        v_s_first = held("v_s_first", [P, FIRST], U8)
+        w1_half = [held("w1_half%d" % u, [P, PACK, PASS // 2], F32) for u in range(2)]
+        w1_bf = [held("w1_bf%d" % b, [P, PASS * PACK], BF16, "slot_" + "fi"[b]) for b in range(BLOCKS)]
+        w1_w = [held("w1_w%d" % b, [P, PASS], U32) for b in range(BLOCKS)]
+        w1_s = [held("w1_s%d" % b, [P, PASS], U8) for b in range(BLOCKS)]
+        h_w = [[held("h_w%d%d" % (b, u), [P, BANK], U32) for u in range(S // BANK)] for b in range(BLOCKS)]
+        h_s = [[held("h_s%d%d" % (b, u), [P, BANK], U8) for u in range(S // BANK)] for b in range(BLOCKS)]
+        warm = held("warm", [P, 2], F32)
+
+        nc.gpsimd.memset(tab_s[:].bitcast(I32), 0)
+        nc.vector.memset(warm[:, 0:1], 1.0)
+        nc.gpsimd.memset(w4_raw_s[:].bitcast(I32), 0)
+        tab2_s = held("tab2_s", [P, T2], U8)
+        nc.gpsimd.memset(tab2_s[:].bitcast(I32), 0)
+        nc.scalar.activation(out=warm[:, 1:2], in_=warm[:, 0:1], func=ACT.Abs_reciprocal_sqrt)
+
+        def load_scales(plane, rows):
+            for q in range(4):
+                src = rows[:, 4 * q : 4 * q + 4, :]
+                n = src.shape[0] * 4
+                nc.sync.dma_start(out=plane[32 * q : 32 * q + n, :].bitcast(I32), in_=src.bitcast(I32))
+
+        def load_w1(dst, c0, width):
+            nc.sync.dma_start(out=dst[:], in_=w1[:, c0 : c0 + width].rearrange("(p j) c -> p j c", j=PACK))
+
+        def load_words(dst, words):
+            nc.sync.dma_start(out=dst[:], in_=words.rearrange("p t i -> p (t i)").bitcast(I32))
+
+        nc.sync.dma_start(idx[:], offs)
+        load_words(tab_w, tab_words[0])
+        load_scales(tab_s, tab_scales)
+        for u in range(2):
+            load_w1(w1_half[u], u * (PASS // 2), PASS // 2)
+        load_scales(w4_raw_s, w4_scales)
+        nc.sync.dma_start(out=w4_raw[:].bitcast(I32), in_=w4_words[0].bitcast(I32))
+        w1_rest = held("w1_rest", [P, PACK, PASS], F32)
+        load_w1(w1_rest, PASS, PASS)
+        nc.sync.dma_start(idx2[:], offs2)
+        load_scales(tab2_s, tab2_scales)
+        tab2_w = [held("tab2_w%d" % b, [P, T2], I32, ("", "hbf2")[b]) for b in range(BLOCKS)]
+        for b in range(BLOCKS):
+            load_words(tab2_w[b], tab2_words[b])
+        mean_t = held("mean_t", [P, S2 // P], F32)
+        with nc.allow_non_contiguous_dma(reason="one value of mean for each partition"):
+            nc.sync.dma_start(out=mean_t[:], in_=mean.rearrange("(c p) -> p c", p=P))
+
+        def gather(dst, table, offsets, c0, c1):
+            nc.vector.tensor_copy(out=dst, in_=table.indirect(offsets[:, c0 // 16 : c1 // 16]))
+
+        v2_w, v2_s = {}, {}
+
+        def gather_words2(g, b, tag):
+            v2_w[g, b] = held("v2_w%d%d" % (g, b), [P, SLICE], U32, tag)
+            gather(v2_w[g, b][:], tab2_w[b][:].bitcast(U32), idx2, g * SLICE, (g + 1) * SLICE)
+
+        def gather_scales2(g, tag):
+            v2_s[g] = held("v2_s%d" % g, [P, SLICE], U8, tag)
+            gather(v2_s[g][:], tab2_s[:], idx2, g * SLICE, (g + 1) * SLICE)
+
+        def w1_order(b):
+            return w1_bf[b][:].rearrange("p (t m j) -> p m j t", t=PACK, j=PACK)
+
+        def quantise_w1(b, t0, t1):
+            nc.vector.quantize_mx(
+                out=w1_w[b][:, t0 * P : t1 * P].bitcast(FP8X4),
+                scales=w1_s[b][:, t0 * P : t1 * P],
+                in_=w1_bf[b][:, t0 * PASS : t1 * PASS],
+            )
+
+        def deal_w4(b):
+            cols = slice(b * PASS, (b + 1) * PASS)
+            nc.vector.tensor_copy(
+                out=w4_w[:].bitcast(U16)[:, cols].rearrange("p (t m) -> p t m", t=PACK),
+                in_=w4_raw[:].bitcast(U16)[:, cols].rearrange("p (m t) -> p t m", t=PACK),
+            )
+            nc.vector.tensor_copy(
+                out=w4_s[:, cols].rearrange("p (t m) -> p t m", t=PACK),
+                in_=w4_raw_s[:, cols].rearrange("p (m t) -> p t m", t=PACK),
+            )
+
+        gather(v_w[:], tab_w[:].bitcast(U32), idx, 0, S)
+        halves = [w1_half[u][:].rearrange("p j (m t) -> p m j t", t=PACK) for u in range(2)]
+        nc.scalar.copy(out=w1_order(0)[:, 0:64], in_=halves[0])
+        nc.scalar.copy(out=w1_order(0)[:, 64 : 64 + SHARE], in_=halves[1][:, 0:SHARE])
+        nc.vector.tensor_copy(out=w1_order(0)[:, 64 + SHARE : 128], in_=halves[1][:, SHARE:64])
+        gather(v_s_first[:], tab_s[:], idx, 0, FIRST)
+        for t in range(PACK):
+            quantise_w1(0, t, t + 1)
+        v_s_rest = held("v_s_rest", [P, S - FIRST], U8, "slot_f")
+        gather(v_s_rest[:], tab_s[:], idx, FIRST, S)
+        deal_w4(0)
+
+        steps = [(b, c) for b in range(BLOCKS) for c in range(CHUNKS)]
+        sq, rr, qq, abank, hbf = {}, {}, {}, {}, {}
+
+        def first_product(tag, words, word_cols, dtype, scales, b, c):
+            bank = psum.tile([P, BANK], F32, name=tag, tag=tag)
+            cols = slice(c * JC, (c + 1) * JC)
+            v_s = v_s_first[:, cols] if c * JC < FIRST else v_s_rest[:, c * JC - FIRST : (c + 1) * JC - FIRST]
+            for t in range(PACK):
+                nc.tensor.matmul_mx(
+                    out=bank[:, t * JC : (t + 1) * JC],
+                    lhsT=words[:, t * P * word_cols : (t + 1) * P * word_cols].bitcast(dtype),
+                    lhsT_scale=scales[:, t * P : (t + 1) * P],
+                    rhs=v_w[:, cols].bitcast(FP8X4),
+                    rhs_scale=v_s,
+                    start=True,
+                    stop=True,
+                )
+            return bank[:].rearrange("p (t n) -> p n t", t=PACK)
+
+        def half(tile, i):
+            return tile[:, (i % 2) * BANK : (i % 2 + 1) * BANK]
+
+        def square_x(i):
+            b, c = steps[i]
+            x = first_product("xy", w1_w[b], 1, FP8X4, w1_s[b], b, c)
+            sq[i] = ring.tile([P, BANK], F32, name="sq")
+            nc.scalar.activation(out=sq[i][:].rearrange("p (n t) -> p n t", t=PACK), in_=x, func=ACT.Square)
+
+        def inverse(i):
+            rr[i] = ring.tile([P, BANK], F32, name="rr")
+            qq[i] = held("qq%d" % i, [P, BANK], F32, "qq%d" % i)
+            r = rr[i][:]
+            nc.scalar.activation(out=r, in_=sq[i][:], func=ACT.Abs_reciprocal_sqrt, bias=1.0)
+            if i in SCALAR_STEPS:
+                nc.scalar.activation(out=qq[i][:], in_=r, func=ACT.Square)
+            else:
+                nc.gpsimd.tensor_tensor(out=qq[i][:], in0=r, in1=r, op=ALU.mult)
+
+        def amplitude(i):
+            b, c = steps[i]
+            abank[i] = first_product(
+                "a", w4_w[:, 2 * b * PASS : 2 * (b + 1) * PASS], 2, FP4X4, w4_s[:, b * PASS : (b + 1) * PASS], b, c
+            )
+
+        def make_h(i):
+            if i % 4 == 0:
+                hbf[i // 4] = held("hbf%d" % (i // 4), [P, 4 * BANK], BF16, "hbf%d" % (i // 4))
+            dst = hbf[i // 4][:, (i % 4) * BANK : (i % 4 + 1) * BANK]
+            nc.vector.tensor_tensor(
+                out=dst.rearrange("p (n t) -> p n t", t=PACK),
+                in0=abank[i],
+                in1=qq[i][:].rearrange("p (n t) -> p n t", t=PACK),
+                op=ALU.mult,
+            )
+
+        def quantise_h(i0, i1):
+            b, u = divmod(i0 // 4, 2)
+            cols = slice((i0 % 4) * JC, ((i1 - 1) % 4 + 1) * JC)
+            nc.vector.quantize_mx(
+                out=h_w[b][u][:, cols].bitcast(FP8X4),
+                scales=h_s[b][u][:, cols],
+                in_=hbf[i0 // 4][:, cols.start * PACK : cols.stop * PACK],
+            )
+
+        n = len(steps)
+        for i in range(n + 5):
+            if i < n:
+                square_x(i)
+            if 0 <= i - 1 < n:
+                inverse(i - 1)
+                amplitude(i - 1)
+            if i - 3 == 8:
+                whole = held("v2_w_second", [P, S2], U32)
+                gather(whole[:], tab2_w[1][:].bitcast(U32), idx2, 0, S2)
+                for g in range(2):
+                    v2_w[g, 1] = whole[:, g * SLICE : (g + 1) * SLICE]
+            if 0 <= i - 3 < n:
+                make_h(i - 3)
+            if i - 4 in (3, 7, 11, 15):
+                quantise_h(i - 7, i - 3)
+            if i == 2:
+                nc.vector.tensor_copy(
+                    out=w1_order(1), in_=w1_rest[:].rearrange("p j (m t) -> p m j t", t=PACK)
+                )
+                deal_w4(1)
+                quantise_w1(1, 0, PACK)
+            if i - 3 == 1:
+                gather_scales2(0, "qq1")
+            if i - 3 == 4:
+                gather_words2(0, 0, "qq4")
+        gather_words2(1, 0, "hbf3")
+        gather_scales2(1, "qq15")
+        nc.scalar.activation(out=warm[:, 1:2], in_=rr[n - 1][:, 0:1], func=ACT.Exp)
+
+        for g in range(S2 // SLICE):
+            for jh in range(S // BANK):
+                for mt in range(g * SLICE // P, (g + 1) * SLICE // P):
+                    rows = slice(mt * P, (mt + 1) * P)
+                    cols = slice(jh * BANK, (jh + 1) * BANK)
+                    local = slice(mt * P - g * SLICE, (mt + 1) * P - g * SLICE)
+                    y = psum.tile([P, BANK], F32, name="xy", tag="xy")
+                    for b in range(BLOCKS):
+                        nc.tensor.matmul_mx(
+                            out=y[:],
+                            lhsT=v2_w[g, b][:, local].bitcast(FP8X4),
+                            lhsT_scale=v2_s[g][4 * b : P, local],
+                            rhs=h_w[b][jh][:].bitcast(FP8X4),
+                            rhs_scale=h_s[b][jh][:],
+                            start=(b == 0),
+                            stop=(b == BLOCKS - 1),
+                        )
+                    power = ring.tile([P, BANK], F32, name="power", bufs=16)
+                    nc.scalar.activation(out=power[:], in_=y[:], func=ACT.Exp, bias=mean_t[:, mt : mt + 1])
+                    nc.sync.dma_start(out=out[rows, cols], in_=power[:])

@@ -26,7 +26,7 @@ BANK = 512
 SLICE = 512
 FIRST = 256
 SHARE = 24
-SCALAR_STEPS = (7, 14)
+SCALAR_STEPS = (0, 1, 9, 10, 11)
 
 
 def tile_list_power_spectrum_emulator_kernel(
@@ -171,7 +171,7 @@ def tile_list_power_spectrum_emulator_kernel(
             nc.scalar.activation(out=sq[i][:].rearrange("p (n t) -> p n t", t=PACK), in_=x, func=ACT.Square)
 
         def inverse(i):
-            rr[i] = ring.tile([P, BANK], F32, name="rr")
+            rr[i] = ring.tile([P, BANK], F32, name="rr", bufs=6)
             qq[i] = held("qq%d" % i, [P, BANK], F32, "qq%d" % i)
             r = rr[i][:]
             nc.scalar.activation(out=r, in_=sq[i][:], func=ACT.Abs_reciprocal_sqrt, bias=1.0)

from contextlib import ExitStack

import concourse.mybir as mybir

K, H, T, S, T2, S2 = 512, 1024, 2048, 1024, 4096, 1024
FLOPS = 2 * K * H * S * 2 + 2 * H * S2 * S

F32 = mybir.dt.float32
BF16 = mybir.dt.bfloat16
I32 = mybir.dt.int32
U32 = mybir.dt.uint32
U16 = mybir.dt.uint16
U8 = mybir.dt.uint8
FP8X4 = mybir.dt.float8_e4m3fn_x4
FP4X4 = mybir.dt.float4_e2m1fn_x4
ACT = mybir.ActivationFunctionType
ALU = mybir.AluOpType

P = 128
PACK = 4
PASS = P * PACK
BLOCKS = H // PASS
JC = 128
CHUNKS = S // JC
BANK = 512
SLICE = 512
FIRST = 256
SHARE = 24
SCALAR_STEPS = (0, 1, 9, 10, 11)


def tile_list_power_spectrum_emulator_kernel(
    tc, tab_words, tab_scales, tab2_words, tab2_scales, w4_words, w4_scales, w1, mean, offs, offs2, out
):
    nc = tc.nc
    with ExitStack() as ctx:
        keep = ctx.enter_context(tc.tile_pool(name="keep", bufs=1))
        ring = ctx.enter_context(tc.tile_pool(name="ring", bufs=4))
        psum = ctx.enter_context(tc.psum_pool(name="psum", bufs=4))

        def held(name, shape, dtype, tag=""):
            return keep.tile(shape, dtype, name=name, tag=tag, align_bytes=64)

        idx = keep.tile([P, S // 16], U16, name="idx")
        idx2 = keep.tile([P, S2 // 16], U16, name="idx2")
        tab_w = held("tab_w", [P, T], I32)
        tab_s = held("tab_s", [P, T], U8)
        w4_raw = held("w4_raw", [P, 2 * H], U8)
        w4_raw_s = held("w4_raw_s", [P, H], U8)
        w4_w = held("w4_w", [P, 2 * H], U8)
        w4_s = held("w4_s", [P, H], U8)
        v_w = held("v_w", [P, S], U32)
        v_s_first = held("v_s_first", [P, FIRST], U8)
        w1_half = [held("w1_half%d" % u, [P, PACK, PASS // 2], F32) for u in range(2)]
        w1_bf = [held("w1_bf%d" % b, [P, PASS * PACK], BF16, "slot_" + "fi"[b]) for b in range(BLOCKS)]
        w1_w = [held("w1_w%d" % b, [P, PASS], U32) for b in range(BLOCKS)]
        w1_s = [held("w1_s%d" % b, [P, PASS], U8) for b in range(BLOCKS)]
        h_w = [[held("h_w%d%d" % (b, u), [P, BANK], U32) for u in range(S // BANK)] for b in range(BLOCKS)]
        h_s = [[held("h_s%d%d" % (b, u), [P, BANK], U8) for u in range(S // BANK)] for b in range(BLOCKS)]
        warm = held("warm", [P, 2], F32)

        nc.gpsimd.memset(tab_s[:].bitcast(I32), 0)
        nc.vector.memset(warm[:, 0:1], 1.0)
        nc.gpsimd.memset(w4_raw_s[:].bitcast(I32), 0)
        tab2_s = held("tab2_s", [P, T2], U8)
        nc.gpsimd.memset(tab2_s[:].bitcast(I32), 0)
        nc.scalar.activation(out=warm[:, 1:2], in_=warm[:, 0:1], func=ACT.Abs_reciprocal_sqrt)

        def load_scales(plane, rows):
            for q in range(4):
                src = rows[:, 4 * q : 4 * q + 4, :]
                n = src.shape[0] * 4
                nc.sync.dma_start(out=plane[32 * q : 32 * q + n, :].bitcast(I32), in_=src.bitcast(I32))

        def load_w1(dst, c0, width):
            nc.sync.dma_start(out=dst[:], in_=w1[:, c0 : c0 + width].rearrange("(p j) c -> p j c", j=PACK))

        def load_words(dst, words):
            nc.sync.dma_start(out=dst[:], in_=words.rearrange("p t i -> p (t i)").bitcast(I32))

        nc.sync.dma_start(idx[:], offs)
        load_words(tab_w, tab_words[0])
        load_scales(tab_s, tab_scales)
        for u in range(2):
            load_w1(w1_half[u], u * (PASS // 2), PASS // 2)
        load_scales(w4_raw_s, w4_scales)
        nc.sync.dma_start(out=w4_raw[:].bitcast(I32), in_=w4_words[0].bitcast(I32))
        w1_rest = held("w1_rest", [P, PACK, PASS], F32)
        load_w1(w1_rest, PASS, PASS)
        nc.sync.dma_start(idx2[:], offs2)
        load_scales(tab2_s, tab2_scales)
        tab2_w = [held("tab2_w%d" % b, [P, T2], I32, ("", "hbf2")[b]) for b in range(BLOCKS)]
        for b in range(BLOCKS):
            load_words(tab2_w[b], tab2_words[b])
        mean_t = held("mean_t", [P, S2 // P], F32)
        with nc.allow_non_contiguous_dma(reason="one value of mean for each partition"):
            nc.sync.dma_start(out=mean_t[:], in_=mean.rearrange("(c p) -> p c", p=P))

        def gather(dst, table, offsets, c0, c1):
            nc.vector.tensor_copy(out=dst, in_=table.indirect(offsets[:, c0 // 16 : c1 // 16]))

        v2_w, v2_s = {}, {}

        def gather_words2(g, b, tag):
            v2_w[g, b] = held("v2_w%d%d" % (g, b), [P, SLICE], U32, tag)
            gather(v2_w[g, b][:], tab2_w[b][:].bitcast(U32), idx2, g * SLICE, (g + 1) * SLICE)

        def gather_scales2(g, tag):
            v2_s[g] = held("v2_s%d" % g, [P, SLICE], U8, tag)
            gather(v2_s[g][:], tab2_s[:], idx2, g * SLICE, (g + 1) * SLICE)

        def w1_order(b):
            return w1_bf[b][:].rearrange("p (t m j) -> p m j t", t=PACK, j=PACK)

        def quantise_w1(b, t0, t1):
            nc.vector.quantize_mx(
                out=w1_w[b][:, t0 * P : t1 * P].bitcast(FP8X4),
                scales=w1_s[b][:, t0 * P : t1 * P],
                in_=w1_bf[b][:, t0 * PASS : t1 * PASS],
            )

        def deal_w4(b):
            cols = slice(b * PASS, (b + 1) * PASS)
            nc.vector.tensor_copy(
                out=w4_w[:].bitcast(U16)[:, cols].rearrange("p (t m) -> p t m", t=PACK),
                in_=w4_raw[:].bitcast(U16)[:, cols].rearrange("p (m t) -> p t m", t=PACK),
            )
            nc.vector.tensor_copy(
                out=w4_s[:, cols].rearrange("p (t m) -> p t m", t=PACK),
                in_=w4_raw_s[:, cols].rearrange("p (m t) -> p t m", t=PACK),
            )

        gather(v_w[:], tab_w[:].bitcast(U32), idx, 0, S)
        halves = [w1_half[u][:].rearrange("p j (m t) -> p m j t", t=PACK) for u in range(2)]
        nc.scalar.copy(out=w1_order(0)[:, 0:64], in_=halves[0])
        nc.scalar.copy(out=w1_order(0)[:, 64 : 64 + SHARE], in_=halves[1][:, 0:SHARE])
        nc.vector.tensor_copy(out=w1_order(0)[:, 64 + SHARE : 128], in_=halves[1][:, SHARE:64])
        gather(v_s_first[:], tab_s[:], idx, 0, FIRST)
        for t in range(PACK):
            quantise_w1(0, t, t + 1)
        v_s_rest = held("v_s_rest", [P, S - FIRST], U8, "slot_f")
        gather(v_s_rest[:], tab_s[:], idx, FIRST, S)
        deal_w4(0)

        steps = [(b, c) for b in range(BLOCKS) for c in range(CHUNKS)]
        sq, rr, qq, abank, hbf = {}, {}, {}, {}, {}

        def first_product(tag, words, word_cols, dtype, scales, b, c):
            bank = psum.tile([P, BANK], F32, name=tag, tag=tag)
            cols = slice(c * JC, (c + 1) * JC)
            v_s = v_s_first[:, cols] if c * JC < FIRST else v_s_rest[:, c * JC - FIRST : (c + 1) * JC - FIRST]
            for t in range(PACK):
                nc.tensor.matmul_mx(
                    out=bank[:, t * JC : (t + 1) * JC],
                    lhsT=words[:, t * P * word_cols : (t + 1) * P * word_cols].bitcast(dtype),
                    lhsT_scale=scales[:, t * P : (t + 1) * P],
                    rhs=v_w[:, cols].bitcast(FP8X4),
                    rhs_scale=v_s,
                    start=True,
                    stop=True,
                )
            return bank[:].rearrange("p (t n) -> p n t", t=PACK)

        def half(tile, i):
            return tile[:, (i % 2) * BANK : (i % 2 + 1) * BANK]

        def square_x(i):
            b, c = steps[i]
            x = first_product("xy", w1_w[b], 1, FP8X4, w1_s[b], b, c)
            sq[i] = ring.tile([P, BANK], F32, name="sq")
            nc.scalar.activation(out=sq[i][:].rearrange("p (n t) -> p n t", t=PACK), in_=x, func=ACT.Square)

        def inverse(i):
            rr[i] = ring.tile([P, BANK], F32, name="rr", bufs=6)
            qq[i] = held("qq%d" % i, [P, BANK], F32, "qq%d" % i)
            r = rr[i][:]
            nc.scalar.activation(out=r, in_=sq[i][:], func=ACT.Abs_reciprocal_sqrt, bias=1.0)
            if i in SCALAR_STEPS:
                nc.scalar.activation(out=qq[i][:], in_=r, func=ACT.Square)
            else:
                nc.gpsimd.tensor_tensor(out=qq[i][:], in0=r, in1=r, op=ALU.mult)

        def amplitude(i):
            b, c = steps[i]
            abank[i] = first_product(
                "a", w4_w[:, 2 * b * PASS : 2 * (b + 1) * PASS], 2, FP4X4, w4_s[:, b * PASS : (b + 1) * PASS], b, c
            )

        def make_h(i):
            if i % 4 == 0:
                hbf[i // 4] = held("hbf%d" % (i // 4), [P, 4 * BANK], BF16, "hbf%d" % (i // 4))
            dst = hbf[i // 4][:, (i % 4) * BANK : (i % 4 + 1) * BANK]
            nc.vector.tensor_tensor(
                out=dst.rearrange("p (n t) -> p n t", t=PACK),
                in0=abank[i],
                in1=qq[i][:].rearrange("p (n t) -> p n t", t=PACK),
                op=ALU.mult,
            )

        def quantise_h(i0, i1):
            b, u = divmod(i0 // 4, 2)
            cols = slice((i0 % 4) * JC, ((i1 - 1) % 4 + 1) * JC)
            nc.vector.quantize_mx(
                out=h_w[b][u][:, cols].bitcast(FP8X4),
                scales=h_s[b][u][:, cols],
                in_=hbf[i0 // 4][:, cols.start * PACK : cols.stop * PACK],
            )

        n = len(steps)
        for i in range(n + 5):
            if i < n:
                square_x(i)
            if 0 <= i - 1 < n:
                inverse(i - 1)
                amplitude(i - 1)
            if i - 3 == 8:
                whole = held("v2_w_second", [P, S2], U32)
                gather(whole[:], tab2_w[1][:].bitcast(U32), idx2, 0, S2)
                for g in range(2):
                    v2_w[g, 1] = whole[:, g * SLICE : (g + 1) * SLICE]
            if 0 <= i - 3 < n:
                make_h(i - 3)
            if i - 4 in (3, 7, 11, 15):
                quantise_h(i - 7, i - 3)
            if i == 2:
                nc.vector.tensor_copy(
                    out=w1_order(1), in_=w1_rest[:].rearrange("p j (m t) -> p m j t", t=PACK)
                )
                deal_w4(1)
                quantise_w1(1, 0, PACK)
            if i - 3 == 1:
                gather_scales2(0, "qq1")
            if i - 3 == 4:
                gather_words2(0, 0, "qq4")
        gather_words2(1, 0, "hbf3")
        gather_scales2(1, "qq15")
        nc.scalar.activation(out=warm[:, 1:2], in_=rr[n - 1][:, 0:1], func=ACT.Exp)

        for g in range(S2 // SLICE):
            for jh in range(S // BANK):
                for mt in range(g * SLICE // P, (g + 1) * SLICE // P):
                    rows = slice(mt * P, (mt + 1) * P)
                    cols = slice(jh * BANK, (jh + 1) * BANK)
                    local = slice(mt * P - g * SLICE, (mt + 1) * P - g * SLICE)
                    y = psum.tile([P, BANK], F32, name="xy", tag="xy")
                    for b in range(BLOCKS):
                        nc.tensor.matmul_mx(
                            out=y[:],
                            lhsT=v2_w[g, b][:, local].bitcast(FP8X4),
                            lhsT_scale=v2_s[g][4 * b : P, local],
                            rhs=h_w[b][jh][:].bitcast(FP8X4),
                            rhs_scale=h_s[b][jh][:],
                            start=(b == 0),
                            stop=(b == BLOCKS - 1),
                        )
                    power = ring.tile([P, BANK], F32, name="power", bufs=16)
                    nc.scalar.activation(out=power[:], in_=y[:], func=ACT.Exp, bias=mean_t[:, mt : mt + 1])
                    nc.sync.dma_start(out=out[rows, cols], in_=power[:])
